import numpy as np
import ml_dtypes


def mxq(x, axis, fmt="e4m3"):
    dtype, down = {"e4m3": (ml_dtypes.float8_e4m3fn, 7), "e5m2": (ml_dtypes.float8_e5m2, 14)}[fmt]
    v = np.moveaxis(np.asarray(x, np.float32).astype(ml_dtypes.bfloat16).astype(np.float64), axis, -1)
    blocks = v.reshape(v.shape[:-1] + (-1, 32))
    amax = np.abs(blocks).max(-1, keepdims=True)
    byte = np.maximum(np.where(amax > 0, np.frexp(amax)[1] - 1 + 127, 0) - down, 1)
    scale = np.exp2(byte - 127.0)
    codes = (blocks / scale).astype(np.float32).astype(dtype).astype(np.float64)
    return np.moveaxis((codes * scale).reshape(v.shape), -1, axis)


WIDE = False


def mx_kscale(k):
    if not WIDE:
        return np.ones(k)
    levels = np.array([10, -10, 5, -5, 0])
    if k % 512:
        return np.exp2(np.random.permutation(np.resize(levels, k // 32))).repeat(32)
    a = np.empty((k // 512, 16))
    for p in range(k // 512):
        a[p, :8] = np.random.permutation(np.resize(levels, 8))
        for g in range(8):
            far = levels[np.abs(levels - a[p, g]) >= 10]
            a[p, g + 8] = far[np.random.randint(len(far))]
    return np.exp2(a.ravel()).repeat(32)


def f64(x):
    return np.asarray(x).astype(np.float64)


def striped(idx):
    return np.tile(idx.reshape(-1, 16).T, (8, 1)).astype(np.uint16)


def unstriped(offs):
    return offs[:16].T.reshape(-1).astype(np.int64)


E2M1 = np.array([0.0, 0.5, 1.0, 1.5, 2.0, 3.0, 4.0, 6.0, -0.0, -0.5, -1.0, -1.5, -2.0, -3.0, -4.0, -6.0])


def pack_weight(w, fmt):
    k, n = w.shape
    w = f64(np.asarray(w, np.float32).astype(ml_dtypes.bfloat16)).reshape(k // 32, 32, n)
    amax = np.abs(w).max(1)
    if fmt == "e4m3":
        byte = np.frexp(amax)[1] - 1 + 127 - 7
    else:
        mant, ex = np.frexp(amax / 6.0)
        byte = np.where(mant > 0.5, ex, ex - 1) + 127
    byte = np.clip(np.where(amax > 0, byte, 1), 1, 254)
    scaled = (w * np.exp2(127.0 - byte)[:, None, :]).reshape(k, n).astype(np.float32)
    by_word = np.ascontiguousarray(scaled.reshape(k // 512, 128, 4, n).transpose(0, 1, 3, 2))
    if fmt == "e4m3":
        words = by_word.astype(ml_dtypes.float8_e4m3fn).view(np.uint8)
    else:
        c = by_word.astype(ml_dtypes.float4_e2m1fn).view(np.uint8) & 0xF
        words = (c[..., 0::2] | (c[..., 1::2] << 4)).reshape(k // 512, 128, 2 * n)
    return np.ascontiguousarray(words), np.ascontiguousarray(byte.astype(np.uint8).reshape(k // 512, 16, n))


def unpack_weight(words, scales, fmt):
    g, _, n = scales.shape
    words = np.ascontiguousarray(words).reshape(g, 128, n, -1)
    if fmt == "e4m3":
        vals = words.view(ml_dtypes.float8_e4m3fn).astype(np.float64)
    else:
        nib = np.empty((g, 128, n, 4), np.uint8)
        nib[..., 0::2] = words & 0xF
        nib[..., 1::2] = words >> 4
        vals = E2M1[nib]
    vals = vals * np.repeat(np.exp2(scales.astype(np.float64) - 127.0), 8, axis=1)[..., None]
    return vals.transpose(0, 1, 3, 2).reshape(g * 512, n)


def gelu(v):
    return 0.5 * v * (1.0 + np.tanh(np.sqrt(2.0 / np.pi) * (v + 0.044715 * v**3)))


def striped8(idx):
    return np.concatenate([v.reshape(-1, 16).T for v in idx]).astype(np.uint16)


def unstriped8(offs):
    return np.stack([offs[16 * g:16 * g + 16].T.reshape(-1) for g in range(8)]).astype(np.int64)


def heads(h, wgt, idx8):
    r = np.arange(h.shape[0])
    return wgt[r // 4 % 128] * h[r[:, None], idx8[r % 512 // 64]]


def put_heads(h, wgs, idx8, t2):
    r = np.arange(h.shape[0])
    page = np.zeros((h.shape[0], t2))
    page[r[:, None], idx8[r % 512 // 64]] = wgs[r // 4 % 128] * h
    return page


T, S, P, T2, K, H, N = 4096, 1024, 512, 1024, 1536, 1024, 512

def setup_inputs():
    n = np.random.standard_normal
    s = mx_kscale(K)[:, None]
    u = mx_kscale(H)[:, None]
    d = {}
    d["tab_words"], d["tab_scales"] = pack_weight(n((K, T)) * s, "e4m3")
    d["offs"] = striped(np.random.permutation(T)[:S])
    d["w1"] = (n((K, H)) / s * u.T / K**0.5).astype(np.float32)
    d["weather"] = np.exp(0.5 * n((H, S))).astype(np.float32)
    d["offs2"] = striped8(np.stack([np.random.permutation(S)[:P] for _ in range(8)]))
    d["wgt"] = np.repeat(np.random.uniform(0.5, 2.0, (8, P)), 16, axis=0).astype(np.float32)
    d["pond"] = (n(H) * u[:, 0]).astype(np.float32)
    d["w2_words"], d["w2_scales"] = pack_weight(n((H, H)) / u * u.T / H**0.5, "e2m1")
    d["w3"] = (n((H, N)) / u / H**0.5).astype(np.float32)
    d["master"] = n(N).astype(np.float32)
    d["offs3"] = striped8(np.stack([np.random.permutation(T2)[:P] for _ in range(8)]))
    d["wgo"] = np.repeat(np.random.uniform(0.5, 2.0, (8, P)), 16, axis=0).astype(np.float32)
    return d

def reference(tab_words, tab_scales, offs, w1, weather, offs2, wgt, pond, w2_words, w2_scales, w3, master, offs3, wgo):
    v = unpack_weight(tab_words, tab_scales, "e4m3")[:, unstriped(offs)]
    h = (mxq(f64(w1), 0, "e4m3").T @ v) * f64(weather)
    x = heads(h, f64(wgt), unstriped8(offs2)) + f64(pond)[:, None]
    w2 = unpack_weight(w2_words, w2_scales, "e2m1")
    top = np.maximum(w2.T @ mxq(x, 0, "e4m3"), x)
    y = (mxq(f64(w3), 0, "e4m3").T @ mxq(top, 0, "e4m3")) + f64(master)[:, None]
    return put_heads(y, f64(wgo), unstriped8(offs3), T2)

@@ -1,0 +1,276 @@
+from contextlib import ExitStack
+
+import concourse.mybir as mybir
+
+T, S, M, T2, K, H, N = 4096, 1024, 512, 1024, 1536, 1024, 512
+FLOPS = 2 * (K * H * S + H * H * M + H * N * M)
+
+F32 = mybir.dt.float32
+BF16 = mybir.dt.bfloat16
+I32 = mybir.dt.int32
+U32 = mybir.dt.uint32
+U16 = mybir.dt.uint16
+U8 = mybir.dt.uint8
+FP8X4 = mybir.dt.float8_e4m3fn_x4
+FP4X4 = mybir.dt.float4_e2m1fn_x4
+MULT = mybir.AluOpType.mult
+MAX = mybir.AluOpType.max
+IDENTITY = mybir.ActivationFunctionType.Identity
+
+P = 128
+PACK = 4
+KP = P * PACK
+BANK = 512
+HALF = M // 2
+QUARTER = M // 4
+PER_COL = 16
+
+
+def tile_list_pond_row_readiness_kernel(
+    tc, tab_words, tab_scales, offs, w1, weather, offs2, wgt, pond, w2_words, w2_scales, w3, master, offs3, wgo, out
+):
+    nc = tc.nc
+    passes1 = K // KP
+    blocks = H // KP
+
+    with ExitStack() as ctx:
+        keep = ctx.enter_context(tc.tile_pool(name="keep", bufs=1))
+        ring = ctx.enter_context(tc.tile_pool(name="ring", bufs=2))
+        psum = ctx.enter_context(tc.psum_pool(name="psum", bufs=1))
+
+        banks = [psum.tile([P, BANK], F32, name=f"bank{i}") for i in range(8)]
+
+        list1 = keep.tile([P, S // PER_COL], U16, name="list1")
+        list2 = keep.tile([P, M // PER_COL], U16, name="list2")
+        list3 = keep.tile([P, M // PER_COL], U16, name="list3")
+        pond_sb = keep.tile([P, blocks, PACK], F32, name="pond_sb")
+        master_sb = keep.tile([P, PACK], F32, name="master_sb")
+        wgt_sb = keep.tile([P, M], F32, name="wgt_sb")
+        wgo_sb = keep.tile([P, M], F32, name="wgo_sb")
+        tab_w = [keep.tile([P, T], I32, name=f"tab_w{a}") for a in range(passes1)]
+        tab_s = keep.tile([P, T], U8, name="tab_s", align_bytes=64)
+        w2_raw = keep.tile([P, blocks * H * 2], U8, name="w2_raw", align_bytes=64)
+        w2s_raw = keep.tile([P, blocks * H], U8, name="w2s_raw", align_bytes=64)
+        w2_c = keep.tile([P, blocks * H * 2], U8, name="w2_c", align_bytes=64)
+        w2_s = keep.tile([P, blocks * H], U8, name="w2_s", align_bytes=64)
+        v_c = [keep.tile([P, S], U32, name=f"v_c{a}", align_bytes=64) for a in range(passes1)]
+        v_s = keep.tile([P, S], U8, name="v_s", align_bytes=64)
+        pages = [keep.tile([P, T2], F32, name=f"page{t}") for t in range(PACK)]
+
+        nc.vector.memset(tab_s[:].bitcast(I32), 0)
+        nc.vector.memset(w2s_raw[:].bitcast(I32), 0)
+
+        def load_weight(w, a, b):
+            raw = ring.tile([P, PACK, KP], F32, name="w_raw", bufs=3)
+            rows = w[a * KP : (a + 1) * KP, b * KP : (b + 1) * KP]
+            nc.sync.dma_start(out=raw[:], in_=rows.rearrange("(p j) c -> p j c", j=PACK))
+            return raw
+
+        def load_table(a):
+            nc.sync.dma_start(out=tab_w[a][:], in_=tab_words[a].rearrange("p t i -> p (t i)").bitcast(I32))
+
+        weather_rows = weather.rearrange("(b p t) j -> b t p j", p=P, t=PACK)
+
+        def load_weather(b, t):
+            we = ring.tile([P, S], F32, name="we", bufs=4)
+            nc.sync.dma_start(out=we[:], in_=weather_rows[b, t])
+            return we
+
+        w1_raw = {}
+        w3_raw = {}
+        we_sb = {}
+        w1_raw[0, 0] = load_weight(w1, 0, 0)
+        nc.sync.dma_start(list1[:], offs)
+        nc.sync.dma_start(list2[:], offs2)
+        nc.sync.dma_start(list3[:], offs3)
+        nc.sync.dma_start(out=pond_sb[:], in_=pond.rearrange("(b p t) -> p b t", p=P, t=PACK))
+        nc.sync.dma_start(out=master_sb[:], in_=master.rearrange("(p t) -> p t", t=PACK))
+        nc.sync.dma_start(
+            out=w2_raw[:].bitcast(I32).rearrange("p (a c) -> p a c", a=blocks),
+            in_=w2_words.bitcast(I32).rearrange("a p c -> p a c"),
+        )
+        w1_raw[1, 0] = load_weight(w1, 1, 0)
+        w1_raw[2, 0] = load_weight(w1, 2, 0)
+        load_table(0)
+        for q in range(4):
+            nc.sync.dma_start(
+                out=tab_s[32 * q : 32 * q + 4 * passes1, :].bitcast(I32),
+                in_=tab_scales[:, 4 * q : 4 * q + 4, :].bitcast(I32),
+            )
+        load_table(1)
+        for q in range(4):
+            nc.sync.dma_start(
+                out=w2s_raw[32 * q : 32 * q + 4, :].bitcast(I32).rearrange("r (a c) -> r a c", a=blocks),
+                in_=w2_scales[:, 4 * q : 4 * q + 4, :].bitcast(I32).rearrange("a r c -> r a c"),
+            )
+        load_table(2)
+        we_sb[0, 0] = load_weather(0, 0)
+        nc.sync.dma_start(out=wgt_sb[:], in_=wgt)
+        we_sb[0, 1] = load_weather(0, 1)
+        w1_raw[0, 1] = load_weight(w1, 0, 1)
+        w1_raw[1, 1] = load_weight(w1, 1, 1)
+        we_sb[0, 2] = load_weather(0, 2)
+        w1_raw[2, 1] = load_weight(w1, 2, 1)
+        we_sb[0, 3] = load_weather(0, 3)
+        for t in range(PACK):
+            we_sb[1, t] = load_weather(1, t)
+        for a in range(blocks):
+            w3_raw[a] = load_weight(w3, a, 0)
+        nc.sync.dma_start(out=wgo_sb[:], in_=wgo)
+
+        def quantize(grouped, codes, scales):
+            nc.vector.quantize_mx(out=codes.bitcast(FP8X4), scales=scales, in_=grouped)
+
+        def quantize_weight(raw, name):
+            grouped = ring.tile([P, KP * PACK], BF16, name="w_bf", align_bytes=64)
+            nc.scalar.copy(
+                out=grouped[:].rearrange("p (t q j) -> p q j t", t=PACK, j=PACK),
+                in_=raw[:].rearrange("p j (q t) -> p q j t", t=PACK),
+            )
+            codes = keep.tile([P, KP], U32, name=name + "_c", align_bytes=64)
+            scales = keep.tile([P, KP], U8, name=name + "_s", align_bytes=64)
+            quantize(grouped[:], codes[:], scales[:])
+            return codes, scales
+
+        def gather_table(a, c0, c1):
+            cols = list1[:, c0 // PER_COL : c1 // PER_COL]
+            nc.vector.tensor_copy(v_c[a][:, c0:c1], tab_w[a][:].bitcast(U32).indirect(cols))
+
+        def stage1_pass(wq, a, t, half):
+            codes, scales = wq
+            rows = slice(t * P, (t + 1) * P)
+            cols = slice(half * BANK, (half + 1) * BANK)
+            nc.tensor.matmul_mx(
+                out=banks[2 * t + half][:],
+                lhsT=codes[:, rows].bitcast(FP8X4),
+                lhsT_scale=scales[:, rows],
+                rhs=v_c[a][:, cols].bitcast(FP8X4),
+                rhs_scale=v_s[4 * a : P, cols],
+                start=(a == 0),
+                stop=(a == passes1 - 1),
+            )
+
+        def weather_product(b, t):
+            h = ring.tile([P, S], F32, name="h", bufs=5)
+            for half in range(2):
+                cols = slice(half * BANK, (half + 1) * BANK)
+                nc.vector.tensor_tensor(h[:, cols], banks[2 * t + half][:], we_sb[b, t][:, cols], MULT)
+            return h
+
+        def pick(h, x, b, t, m0, m1):
+            cols = list2[:, m0 // PER_COL : m1 // PER_COL]
+            nc.vector.tensor_tensor(x[:, t, :], h[:].indirect(cols), wgt_sb[:, m0:m1], MULT)
+            nc.scalar.activation(x[:, t, :], x[:, t, :], IDENTITY, bias=pond_sb[:, b, t : t + 1])
+
+        x_c = [keep.tile([P, M], U32, name=f"x_c{b}", align_bytes=64) for b in range(blocks)]
+        x_s = [keep.tile([P, M], U8, name=f"x_s{b}", align_bytes=64) for b in range(blocks)]
+        top_c = [keep.tile([P, M], U32, name=f"top_c{b}", align_bytes=64) for b in range(blocks)]
+        top_s = [keep.tile([P, M], U8, name=f"top_s{b}", align_bytes=64) for b in range(blocks)]
+
+        def quantize_x(x, b, m0, m1):
+            grouped = ring.tile([P, (m1 - m0) * PACK], BF16, name="x_bf", align_bytes=64)
+            nc.scalar.copy(
+                out=grouped[:].rearrange("p (c i t) -> p c t i", i=4, t=PACK),
+                in_=x[:].rearrange("p t (c i) -> p c t i", i=4),
+            )
+            quantize(grouped[:], x_c[b][:, m0:m1], x_s[b][:, m0:m1])
+
+        def stage2_pass(a, bo, quarter):
+            cols = slice(quarter * QUARTER, (quarter + 1) * QUARTER)
+            bank = banks[2 * quarter + bo]
+            for t in range(PACK):
+                g = (a * blocks + bo) * PACK + t
+                nc.tensor.matmul_mx(
+                    out=bank[:, t * QUARTER : (t + 1) * QUARTER],
+                    lhsT=w2_c[:, g * 2 * P : (g + 1) * 2 * P].bitcast(FP4X4),
+                    lhsT_scale=w2_s[:, g * P : (g + 1) * P],
+                    rhs=x_c[a][:, cols].bitcast(FP8X4),
+                    rhs_scale=x_s[a][:, cols],
+                    start=(a == 0 and t == 0),
+                    stop=(a == blocks - 1 and t == PACK - 1),
+                )
+
+        w1_q = {(a, 0): quantize_weight(w1_raw[a, 0], f"w1q{a}0") for a in range(passes1)}
+        nc.vector.tensor_copy(
+            out=w2_c[:].rearrange("p (g t q e) -> p g t q e", t=PACK, q=P, e=2),
+            in_=w2_raw[:].rearrange("p (g q t e) -> p g t q e", t=PACK, q=P, e=2),
+        )
+        for t in range(PACK):
+            nc.vector.memset(pages[t][:], 0.0)
+        gather_table(0, 0, S)
+        nc.vector.tensor_copy(v_s[:], tab_s[:].indirect(list1[:]))
+        gather_table(1, 0, S)
+        nc.vector.tensor_copy(
+            out=w2_s[:].rearrange("p (g t q) -> p g t q", t=PACK, q=P),
+            in_=w2s_raw[:].rearrange("p (g q t) -> p g t q", t=PACK, q=P),
+        )
+        gather_table(2, 0, BANK)
+        gather_table(2, BANK, S)
+        for a in range(passes1):
+            for t in range(PACK):
+                for half in range(2):
+                    stage1_pass(w1_q[a, 0], a, t, half)
+
+        x0 = keep.tile([P, PACK, M], F32, name="x0")
+        for t in range(PACK):
+            h = weather_product(0, t)
+            pick(h, x0, 0, t, 0, M)
+            if t >= 1:
+                w1_q[t - 1, 1] = quantize_weight(w1_raw[t - 1, 1], f"w1q{t - 1}1")
+        for a in range(passes1):
+            for t in range(PACK):
+                for half in range(2):
+                    stage1_pass(w1_q[a, 1], a, t, half)
+        quantize_x(x0, 0, 0, M)
+
+        hs = [weather_product(1, t) for t in range(PACK)]
+        for quarter in range(4):
+            for bo in range(blocks):
+                stage2_pass(0, bo, quarter)
+        x1 = [keep.tile([P, PACK, HALF], F32, name=f"x1_{half}") for half in range(2)]
+        for half in range(2):
+            for t in range(PACK):
+                pick(hs[t], x1[half], 1, t, half * HALF, (half + 1) * HALF)
+            quantize_x(x1[half], 1, half * HALF, (half + 1) * HALF)
+        w3_q = [quantize_weight(w3_raw[a], f"w3q{a}") for a in range(blocks)]
+
+        out_rows = out.rearrange("(p t) c -> t p c", t=PACK)
+        for half in range(2):
+            m0 = half * HALF
+            tops = [ring.tile([P, HALF * PACK], BF16, name="top_bf", align_bytes=64) for bo in range(blocks)]
+            for part in range(2):
+                quarter = 2 * half + part
+                for bo in range(blocks):
+                    stage2_pass(1, bo, quarter)
+                    if bo == 0:
+                        x_part = x0[:, :, quarter * QUARTER : (quarter + 1) * QUARTER]
+                    else:
+                        x_part = x1[half][:, :, part * QUARTER : (part + 1) * QUARTER]
+                    nc.vector.tensor_tensor(
+                        tops[bo][:, part * BANK : (part + 1) * BANK].rearrange("p (c i t) -> p c t i", i=4, t=PACK),
+                        banks[2 * quarter + bo][:].rearrange("p (t c i) -> p c t i", t=PACK, i=4),
+                        x_part.rearrange("p t (c i) -> p c t i", i=4),
+                        MAX,
+                    )
+            for bo in range(blocks):
+                quantize(tops[bo][:], top_c[bo][:, m0 : m0 + HALF], top_s[bo][:, m0 : m0 + HALF])
+            for t in range(PACK):
+                bank = banks[4 * half + t]
+                rows = slice(t * P, (t + 1) * P)
+                for a in range(blocks):
+                    codes, scales = w3_q[a]
+                    nc.tensor.matmul_mx(
+                        out=bank[:, 0:HALF],
+                        lhsT=codes[:, rows].bitcast(FP8X4),
+                        lhsT_scale=scales[:, rows],
+                        rhs=top_c[a][:, m0 : m0 + HALF].bitcast(FP8X4),
+                        rhs_scale=top_s[a][:, m0 : m0 + HALF],
+                        start=(a == 0),
+                        stop=(a == blocks - 1),
+                    )
+                y = ring.tile([P, HALF], F32, name="y", bufs=4)
+                nc.scalar.activation(y[:], bank[:, 0:HALF], IDENTITY, bias=master_sb[:, t : t + 1])
+                cols = list3[:, m0 // PER_COL : (m0 + HALF) // PER_COL]
+                nc.vector.tensor_tensor(pages[t][:].indirect(cols), y[:], wgo_sb[:, m0 : m0 + HALF], MULT)
+                if half == 1:
+                    nc.sync.dma_start(out=out_rows[t], in_=pages[t][:])

@@ -47,7 +47,7 @@ def tile_list_pond_row_readiness_kernel(
         master_sb = keep.tile([P, PACK], F32, name="master_sb")
         wgt_sb = keep.tile([P, M], F32, name="wgt_sb")
         wgo_sb = keep.tile([P, M], F32, name="wgo_sb")
-        tab_w = [keep.tile([P, T], I32, name=f"tab_w{a}") for a in range(passes1)]
+        tab_w = [ring.tile([P, T], I32, name=f"tab_w{a}", tag="big", bufs=passes1) for a in range(passes1)]
         tab_s = keep.tile([P, T], U8, name="tab_s", align_bytes=64)
         w2_raw = keep.tile([P, blocks * H * 2], U8, name="w2_raw", align_bytes=64)
         w2s_raw = keep.tile([P, blocks * H], U8, name="w2s_raw", align_bytes=64)
@@ -71,14 +71,13 @@ def tile_list_pond_row_readiness_kernel(
 
         weather_rows = weather.rearrange("(b p t) j -> b t p j", p=P, t=PACK)
 
+        we_sb = [keep.tile([P, PACK, S], F32, name="we0"), ring.tile([P, PACK, S], F32, name="we1", tag="big", bufs=passes1)]
+
         def load_weather(b, t):
-            we = ring.tile([P, S], F32, name="we", bufs=4)
-            nc.sync.dma_start(out=we[:], in_=weather_rows[b, t])
-            return we
+            nc.sync.dma_start(out=we_sb[b][:, t, :], in_=weather_rows[b, t])
 
         w1_raw = {}
         w3_raw = {}
-        we_sb = {}
         w1_raw[0, 0] = load_weight(w1, 0, 0)
         nc.sync.dma_start(list1[:], offs)
         nc.sync.dma_start(list2[:], offs2)
@@ -91,6 +90,11 @@ def tile_list_pond_row_readiness_kernel(
         )
         w1_raw[1, 0] = load_weight(w1, 1, 0)
         w1_raw[2, 0] = load_weight(w1, 2, 0)
+        for q in range(4):
+            nc.sync.dma_start(
+                out=w2s_raw[32 * q : 32 * q + 4, :].bitcast(I32).rearrange("r (a c) -> r a c", a=blocks),
+                in_=w2_scales[:, 4 * q : 4 * q + 4, :].bitcast(I32).rearrange("a r c -> r a c"),
+            )
         load_table(0)
         for q in range(4):
             nc.sync.dma_start(
@@ -98,38 +102,38 @@ def tile_list_pond_row_readiness_kernel(
                 in_=tab_scales[:, 4 * q : 4 * q + 4, :].bitcast(I32),
             )
         load_table(1)
-        for q in range(4):
-            nc.sync.dma_start(
-                out=w2s_raw[32 * q : 32 * q + 4, :].bitcast(I32).rearrange("r (a c) -> r a c", a=blocks),
-                in_=w2_scales[:, 4 * q : 4 * q + 4, :].bitcast(I32).rearrange("a r c -> r a c"),
-            )
         load_table(2)
-        we_sb[0, 0] = load_weather(0, 0)
+        load_weather(0, 0)
         nc.sync.dma_start(out=wgt_sb[:], in_=wgt)
-        we_sb[0, 1] = load_weather(0, 1)
+        load_weather(0, 1)
         w1_raw[0, 1] = load_weight(w1, 0, 1)
+        load_weather(0, 2)
         w1_raw[1, 1] = load_weight(w1, 1, 1)
-        we_sb[0, 2] = load_weather(0, 2)
         w1_raw[2, 1] = load_weight(w1, 2, 1)
-        we_sb[0, 3] = load_weather(0, 3)
-        for t in range(PACK):
-            we_sb[1, t] = load_weather(1, t)
-        for a in range(blocks):
-            w3_raw[a] = load_weight(w3, a, 0)
+        load_weather(0, 3)
+        load_weather(1, 0)
+        load_weather(1, 1)
+        w3_raw[0] = load_weight(w3, 0, 0)
+        load_weather(1, 2)
+        load_weather(1, 3)
+        w3_raw[1] = load_weight(w3, 1, 0)
         nc.sync.dma_start(out=wgo_sb[:], in_=wgo)
 
         def quantize(grouped, codes, scales):
             nc.vector.quantize_mx(out=codes.bitcast(FP8X4), scales=scales, in_=grouped)
 
         def quantize_weight(raw, name):
-            grouped = ring.tile([P, KP * PACK], BF16, name="w_bf", align_bytes=64)
-            nc.scalar.copy(
-                out=grouped[:].rearrange("p (t q j) -> p q j t", t=PACK, j=PACK),
-                in_=raw[:].rearrange("p j (q t) -> p q j t", t=PACK),
-            )
             codes = keep.tile([P, KP], U32, name=name + "_c", align_bytes=64)
             scales = keep.tile([P, KP], U8, name=name + "_s", align_bytes=64)
-            quantize(grouped[:], codes[:], scales[:])
+            for u in range(2):
+                grouped = ring.tile([P, 2 * KP], BF16, name="w_bf", bufs=4, align_bytes=64)
+                nc.scalar.activation(
+                    grouped[:].rearrange("p (e q j) -> p q j e", e=2, j=PACK),
+                    raw[:].rearrange("p j (q t) -> p q j t", t=PACK)[:, :, :, 2 * u : 2 * u + 2],
+                    IDENTITY,
+                )
+                cols = slice(2 * u * P, 2 * (u + 1) * P)
+                quantize(grouped[:], codes[:, cols], scales[:, cols])
             return codes, scales
 
         def gather_table(a, c0, c1):
@@ -154,13 +158,15 @@ def tile_list_pond_row_readiness_kernel(
             h = ring.tile([P, S], F32, name="h", bufs=5)
             for half in range(2):
                 cols = slice(half * BANK, (half + 1) * BANK)
-                nc.vector.tensor_tensor(h[:, cols], banks[2 * t + half][:], we_sb[b, t][:, cols], MULT)
+                nc.vector.tensor_tensor(h[:, cols], banks[2 * t + half][:], we_sb[b][:, t, cols], MULT)
             return h
 
-        def pick(h, x, b, t, m0, m1):
+        def pick(h, picked, t, m0, m1):
             cols = list2[:, m0 // PER_COL : m1 // PER_COL]
-            nc.vector.tensor_tensor(x[:, t, :], h[:].indirect(cols), wgt_sb[:, m0:m1], MULT)
-            nc.scalar.activation(x[:, t, :], x[:, t, :], IDENTITY, bias=pond_sb[:, b, t : t + 1])
+            nc.vector.tensor_tensor(picked[:, t, :], h[:].indirect(cols), wgt_sb[:, m0:m1], MULT)
+
+        def add_pond(x, picked, b, t):
+            nc.scalar.activation(x[:, t, :], picked[:, t, :], IDENTITY, bias=pond_sb[:, b, t : t + 1])
 
         x_c = [keep.tile([P, M], U32, name=f"x_c{b}", align_bytes=64) for b in range(blocks)]
         x_s = [keep.tile([P, M], U8, name=f"x_s{b}", align_bytes=64) for b in range(blocks)]
@@ -171,7 +177,7 @@ def tile_list_pond_row_readiness_kernel(
             grouped = ring.tile([P, (m1 - m0) * PACK], BF16, name="x_bf", align_bytes=64)
             nc.scalar.copy(
                 out=grouped[:].rearrange("p (c i t) -> p c t i", i=4, t=PACK),
-                in_=x[:].rearrange("p t (c i) -> p c t i", i=4),
+                in_=x.rearrange("p t (c i) -> p c t i", i=4),
             )
             quantize(grouped[:], x_c[b][:, m0:m1], x_s[b][:, m0:m1])
 
@@ -190,20 +196,20 @@ def tile_list_pond_row_readiness_kernel(
                     stop=(a == blocks - 1 and t == PACK - 1),
                 )
 
-        w1_q = {(a, 0): quantize_weight(w1_raw[a, 0], f"w1q{a}0") for a in range(passes1)}
         nc.vector.tensor_copy(
             out=w2_c[:].rearrange("p (g t q e) -> p g t q e", t=PACK, q=P, e=2),
             in_=w2_raw[:].rearrange("p (g q t e) -> p g t q e", t=PACK, q=P, e=2),
+        )
+        w1_q = {(a, 0): quantize_weight(w1_raw[a, 0], f"w1q{a}0") for a in range(passes1)}
+        nc.vector.tensor_copy(
+            out=w2_s[:].rearrange("p (g t q) -> p g t q", t=PACK, q=P),
+            in_=w2s_raw[:].rearrange("p (g q t) -> p g t q", t=PACK, q=P),
         )
         for t in range(PACK):
             nc.vector.memset(pages[t][:], 0.0)
         gather_table(0, 0, S)
         nc.vector.tensor_copy(v_s[:], tab_s[:].indirect(list1[:]))
         gather_table(1, 0, S)
-        nc.vector.tensor_copy(
-            out=w2_s[:].rearrange("p (g t q) -> p g t q", t=PACK, q=P),
-            in_=w2s_raw[:].rearrange("p (g q t) -> p g t q", t=PACK, q=P),
-        )
         gather_table(2, 0, BANK)
         gather_table(2, BANK, S)
         for a in range(passes1):
@@ -211,28 +217,38 @@ def tile_list_pond_row_readiness_kernel(
                 for half in range(2):
                     stage1_pass(w1_q[a, 0], a, t, half)
 
-        x0 = keep.tile([P, PACK, M], F32, name="x0")
+        picked0 = keep.tile([P, PACK, M], F32, name="picked0")
         for t in range(PACK):
             h = weather_product(0, t)
-            pick(h, x0, 0, t, 0, M)
             if t >= 1:
                 w1_q[t - 1, 1] = quantize_weight(w1_raw[t - 1, 1], f"w1q{t - 1}1")
+            pick(h, picked0[:], t, 0, M)
         for a in range(passes1):
             for t in range(PACK):
                 for half in range(2):
                     stage1_pass(w1_q[a, 1], a, t, half)
+        x0 = w1_raw[passes1 - 1, 1][:]
+        for t in range(PACK):
+            add_pond(x0, picked0[:], 0, t)
         quantize_x(x0, 0, 0, M)
+        w3_q = [quantize_weight(w3_raw[0], "w3q0")]
 
-        hs = [weather_product(1, t) for t in range(PACK)]
+        x1_first = keep.tile([P, PACK, HALF], F32, name="x1_first")
+        x1 = [x1_first[:], we_sb[1][:, PACK - 1, :].rearrange("p (t m) -> p t m", t=PACK)]
+        hs = []
+        for t in range(PACK):
+            hs.append(weather_product(1, t))
+            pick(hs[t], x1[0], t, 0, HALF)
+            add_pond(x1[0], x1[0], 1, t)
         for quarter in range(4):
             for bo in range(blocks):
                 stage2_pass(0, bo, quarter)
-        x1 = [keep.tile([P, PACK, HALF], F32, name=f"x1_{half}") for half in range(2)]
-        for half in range(2):
-            for t in range(PACK):
-                pick(hs[t], x1[half], 1, t, half * HALF, (half + 1) * HALF)
-            quantize_x(x1[half], 1, half * HALF, (half + 1) * HALF)
-        w3_q = [quantize_weight(w3_raw[a], f"w3q{a}") for a in range(blocks)]
+        quantize_x(x1[0], 1, 0, HALF)
+        for t in range(PACK):
+            pick(hs[t], x1[1], t, HALF, M)
+            add_pond(x1[1], x1[1], 1, t)
+        quantize_x(x1[1], 1, HALF, M)
+        w3_q.append(quantize_weight(w3_raw[1], "w3q1"))
 
         out_rows = out.rearrange("(p t) c -> t p c", t=PACK)
         for half in range(2):

@@ -24,6 +24,7 @@ BANK = 512
 HALF = M // 2
 QUARTER = M // 4
 PER_COL = 16
+PITCH = S + HALF
 
 
 def tile_list_pond_row_readiness_kernel(
@@ -47,7 +48,7 @@ def tile_list_pond_row_readiness_kernel(
         master_sb = keep.tile([P, PACK], F32, name="master_sb")
         wgt_sb = keep.tile([P, M], F32, name="wgt_sb")
         wgo_sb = keep.tile([P, M], F32, name="wgo_sb")
-        tab_w = [ring.tile([P, T], I32, name=f"tab_w{a}", tag="big", bufs=passes1) for a in range(passes1)]
+        tab_w = [keep.tile([P, T], I32, name=f"tab_w{a}", tag=f"tab_w{a}") for a in range(passes1)]
         tab_s = keep.tile([P, T], U8, name="tab_s", align_bytes=64)
         w2_raw = keep.tile([P, blocks * H * 2], U8, name="w2_raw", align_bytes=64)
         w2s_raw = keep.tile([P, blocks * H], U8, name="w2s_raw", align_bytes=64)
@@ -71,10 +72,26 @@ def tile_list_pond_row_readiness_kernel(
 
         weather_rows = weather.rearrange("(b p t) j -> b t p j", p=P, t=PACK)
 
-        we_sb = [keep.tile([P, PACK, S], F32, name="we0"), ring.tile([P, PACK, S], F32, name="we1", tag="big", bufs=passes1)]
+        we0 = keep.tile([P, PACK * S + M], F32, name="we0")
+        we1 = keep.tile([P, PACK * PITCH + QUARTER], F32, name="we1", tag="tab_w0")
+        we_sb = [
+            we0[:, 0 : PACK * S].rearrange("p (t j) -> p t j", t=PACK),
+            we1[:, 0 : PACK * PITCH].rearrange("p (t j) -> p t j", t=PACK),
+        ]
 
         def load_weather(b, t):
-            nc.sync.dma_start(out=we_sb[b][:, t, :], in_=weather_rows[b, t])
+            nc.sync.dma_start(out=we_sb[b][:, t, 0:S], in_=weather_rows[b, t])
+
+        for q in range(4):
+            nc.gpsimd.dma_start(
+                out=tab_s[32 * q : 32 * q + 4 * passes1, :].bitcast(I32),
+                in_=tab_scales[:, 4 * q : 4 * q + 4, :].bitcast(I32),
+            )
+        for q in range(4):
+            nc.gpsimd.dma_start(
+                out=w2s_raw[32 * q : 32 * q + 4, :].bitcast(I32).rearrange("r (a c) -> r a c", a=blocks),
+                in_=w2_scales[:, 4 * q : 4 * q + 4, :].bitcast(I32).rearrange("a r c -> r a c"),
+            )
 
         w1_raw = {}
         w3_raw = {}
@@ -90,17 +107,7 @@ def tile_list_pond_row_readiness_kernel(
         )
         w1_raw[1, 0] = load_weight(w1, 1, 0)
         w1_raw[2, 0] = load_weight(w1, 2, 0)
-        for q in range(4):
-            nc.sync.dma_start(
-                out=w2s_raw[32 * q : 32 * q + 4, :].bitcast(I32).rearrange("r (a c) -> r a c", a=blocks),
-                in_=w2_scales[:, 4 * q : 4 * q + 4, :].bitcast(I32).rearrange("a r c -> r a c"),
-            )
         load_table(0)
-        for q in range(4):
-            nc.sync.dma_start(
-                out=tab_s[32 * q : 32 * q + 4 * passes1, :].bitcast(I32),
-                in_=tab_scales[:, 4 * q : 4 * q + 4, :].bitcast(I32),
-            )
         load_table(1)
         load_table(2)
         load_weather(0, 0)
@@ -109,8 +116,8 @@ def tile_list_pond_row_readiness_kernel(
         w1_raw[0, 1] = load_weight(w1, 0, 1)
         load_weather(0, 2)
         w1_raw[1, 1] = load_weight(w1, 1, 1)
-        w1_raw[2, 1] = load_weight(w1, 2, 1)
         load_weather(0, 3)
+        w1_raw[2, 1] = load_weight(w1, 2, 1)
         load_weather(1, 0)
         load_weather(1, 1)
         w3_raw[0] = load_weight(w3, 0, 0)
@@ -217,29 +224,34 @@ def tile_list_pond_row_readiness_kernel(
                 for half in range(2):
                     stage1_pass(w1_q[a, 0], a, t, half)
 
-        picked0 = keep.tile([P, PACK, M], F32, name="picked0")
+        picked0 = we0[:, M:].rearrange("p (t j) -> p t j", t=PACK)[:, :, S - M :]
+        hs = [weather_product(0, 0)]
         for t in range(PACK):
-            h = weather_product(0, t)
+            if t + 1 < PACK:
+                hs.append(weather_product(0, t + 1))
             if t >= 1:
                 w1_q[t - 1, 1] = quantize_weight(w1_raw[t - 1, 1], f"w1q{t - 1}1")
-            pick(h, picked0[:], t, 0, M)
+            pick(hs[t], picked0, t, 0, M)
         for a in range(passes1):
             for t in range(PACK):
                 for half in range(2):
                     stage1_pass(w1_q[a, 1], a, t, half)
         x0 = w1_raw[passes1 - 1, 1][:]
         for t in range(PACK):
-            add_pond(x0, picked0[:], 0, t)
+            add_pond(x0, picked0, 0, t)
         quantize_x(x0, 0, 0, M)
         w3_q = [quantize_weight(w3_raw[0], "w3q0")]
 
+        last = (PACK - 1) * PITCH + QUARTER
+        picked1 = we1[:, QUARTER:].rearrange("p (t j) -> p t j", t=PACK)[:, :, S:]
         x1_first = keep.tile([P, PACK, HALF], F32, name="x1_first")
-        x1 = [x1_first[:], we_sb[1][:, PACK - 1, :].rearrange("p (t m) -> p t m", t=PACK)]
-        hs = []
+        x1 = [x1_first[:], we1[:, last : last + PACK * HALF].rearrange("p (t m) -> p t m", t=PACK)]
+        hs = [weather_product(1, 0)]
         for t in range(PACK):
-            hs.append(weather_product(1, t))
-            pick(hs[t], x1[0], t, 0, HALF)
-            add_pond(x1[0], x1[0], 1, t)
+            if t + 1 < PACK:
+                hs.append(weather_product(1, t + 1))
+            pick(hs[t], picked1, t, 0, HALF)
+            add_pond(x1[0], picked1, 1, t)
         for quarter in range(4):
             for bo in range(blocks):
                 stage2_pass(0, bo, quarter)

from contextlib import ExitStack

import concourse.mybir as mybir

T, S, M, T2, K, H, N = 4096, 1024, 512, 1024, 1536, 1024, 512
FLOPS = 2 * (K * H * S + H * H * M + H * N * M)

F32 = mybir.dt.float32
BF16 = mybir.dt.bfloat16
I32 = mybir.dt.int32
U32 = mybir.dt.uint32
U16 = mybir.dt.uint16
U8 = mybir.dt.uint8
FP8X4 = mybir.dt.float8_e4m3fn_x4
FP4X4 = mybir.dt.float4_e2m1fn_x4
MULT = mybir.AluOpType.mult
MAX = mybir.AluOpType.max
IDENTITY = mybir.ActivationFunctionType.Identity

P = 128
PACK = 4
KP = P * PACK
BANK = 512
HALF = M // 2
QUARTER = M // 4
PER_COL = 16
PITCH = S + HALF


def tile_list_pond_row_readiness_kernel(
    tc, tab_words, tab_scales, offs, w1, weather, offs2, wgt, pond, w2_words, w2_scales, w3, master, offs3, wgo, out
):
    nc = tc.nc
    passes1 = K // KP
    blocks = H // KP

    with ExitStack() as ctx:
        keep = ctx.enter_context(tc.tile_pool(name="keep", bufs=1))
        ring = ctx.enter_context(tc.tile_pool(name="ring", bufs=2))
        psum = ctx.enter_context(tc.psum_pool(name="psum", bufs=1))

        banks = [psum.tile([P, BANK], F32, name=f"bank{i}") for i in range(8)]

        list1 = keep.tile([P, S // PER_COL], U16, name="list1")
        list2 = keep.tile([P, M // PER_COL], U16, name="list2")
        list3 = keep.tile([P, M // PER_COL], U16, name="list3")
        pond_sb = keep.tile([P, blocks, PACK], F32, name="pond_sb")
        master_sb = keep.tile([P, PACK], F32, name="master_sb")
        wgt_sb = keep.tile([P, M], F32, name="wgt_sb")
        wgo_sb = keep.tile([P, M], F32, name="wgo_sb")
        tab_w = [keep.tile([P, T], I32, name=f"tab_w{a}", tag=f"tab_w{a}") for a in range(passes1)]
        tab_s = keep.tile([P, T], U8, name="tab_s", align_bytes=64)
        w2_raw = keep.tile([P, blocks * H * 2], U8, name="w2_raw", align_bytes=64)
        w2s_raw = keep.tile([P, blocks * H], U8, name="w2s_raw", align_bytes=64)
        w2_c = keep.tile([P, blocks * H * 2], U8, name="w2_c", align_bytes=64)
        w2_s = keep.tile([P, blocks * H], U8, name="w2_s", align_bytes=64)
        v_c = [keep.tile([P, S], U32, name=f"v_c{a}", align_bytes=64) for a in range(passes1)]
        v_s = keep.tile([P, S], U8, name="v_s", align_bytes=64)
        pages = [keep.tile([P, T2], F32, name=f"page{t}") for t in range(PACK)]

        nc.vector.memset(tab_s[:].bitcast(I32), 0)
        nc.vector.memset(w2s_raw[:].bitcast(I32), 0)

        def load_weight(w, a, b):
            raw = ring.tile([P, PACK, KP], F32, name="w_raw", bufs=3)
            rows = w[a * KP : (a + 1) * KP, b * KP : (b + 1) * KP]
            nc.sync.dma_start(out=raw[:], in_=rows.rearrange("(p j) c -> p j c", j=PACK))
            return raw

        def load_table(a):
            nc.sync.dma_start(out=tab_w[a][:], in_=tab_words[a].rearrange("p t i -> p (t i)").bitcast(I32))

        weather_rows = weather.rearrange("(b p t) j -> b t p j", p=P, t=PACK)

        we0 = keep.tile([P, PACK * S + M], F32, name="we0")
        we1 = keep.tile([P, PACK * PITCH + QUARTER], F32, name="we1", tag="tab_w0")
        we_sb = [
            we0[:, 0 : PACK * S].rearrange("p (t j) -> p t j", t=PACK),
            we1[:, 0 : PACK * PITCH].rearrange("p (t j) -> p t j", t=PACK),
        ]

        def load_weather(b, t):
            nc.sync.dma_start(out=we_sb[b][:, t, 0:S], in_=weather_rows[b, t])

        for q in range(4):
            nc.gpsimd.dma_start(
                out=tab_s[32 * q : 32 * q + 4 * passes1, :].bitcast(I32),
                in_=tab_scales[:, 4 * q : 4 * q + 4, :].bitcast(I32),
            )
        for q in range(4):
            nc.gpsimd.dma_start(
                out=w2s_raw[32 * q : 32 * q + 4, :].bitcast(I32).rearrange("r (a c) -> r a c", a=blocks),
                in_=w2_scales[:, 4 * q : 4 * q + 4, :].bitcast(I32).rearrange("a r c -> r a c"),
            )

        w1_raw = {}
        w3_raw = {}
        w1_raw[0, 0] = load_weight(w1, 0, 0)
        nc.sync.dma_start(list1[:], offs)
        nc.sync.dma_start(list2[:], offs2)
        nc.sync.dma_start(list3[:], offs3)
        nc.sync.dma_start(out=pond_sb[:], in_=pond.rearrange("(b p t) -> p b t", p=P, t=PACK))
        nc.sync.dma_start(out=master_sb[:], in_=master.rearrange("(p t) -> p t", t=PACK))
        nc.sync.dma_start(
            out=w2_raw[:].bitcast(I32).rearrange("p (a c) -> p a c", a=blocks),
            in_=w2_words.bitcast(I32).rearrange("a p c -> p a c"),
        )
        w1_raw[1, 0] = load_weight(w1, 1, 0)
        w1_raw[2, 0] = load_weight(w1, 2, 0)
        load_table(0)
        load_table(1)
        load_table(2)
        load_weather(0, 0)
        nc.sync.dma_start(out=wgt_sb[:], in_=wgt)
        load_weather(0, 1)
        w1_raw[0, 1] = load_weight(w1, 0, 1)
        load_weather(0, 2)
        w1_raw[1, 1] = load_weight(w1, 1, 1)
        load_weather(0, 3)
        w1_raw[2, 1] = load_weight(w1, 2, 1)
        load_weather(1, 0)
        load_weather(1, 1)
        w3_raw[0] = load_weight(w3, 0, 0)
        load_weather(1, 2)
        load_weather(1, 3)
        w3_raw[1] = load_weight(w3, 1, 0)
        nc.sync.dma_start(out=wgo_sb[:], in_=wgo)

        def quantize(grouped, codes, scales):
            nc.vector.quantize_mx(out=codes.bitcast(FP8X4), scales=scales, in_=grouped)

        def quantize_weight(raw, name):
            codes = keep.tile([P, KP], U32, name=name + "_c", align_bytes=64)
            scales = keep.tile([P, KP], U8, name=name + "_s", align_bytes=64)
            for u in range(2):
                grouped = ring.tile([P, 2 * KP], BF16, name="w_bf", bufs=4, align_bytes=64)
                nc.scalar.activation(
                    grouped[:].rearrange("p (e q j) -> p q j e", e=2, j=PACK),
                    raw[:].rearrange("p j (q t) -> p q j t", t=PACK)[:, :, :, 2 * u : 2 * u + 2],
                    IDENTITY,
                )
                cols = slice(2 * u * P, 2 * (u + 1) * P)
                quantize(grouped[:], codes[:, cols], scales[:, cols])
            return codes, scales

        def gather_table(a, c0, c1):
            cols = list1[:, c0 // PER_COL : c1 // PER_COL]
            nc.vector.tensor_copy(v_c[a][:, c0:c1], tab_w[a][:].bitcast(U32).indirect(cols))

        def stage1_pass(wq, a, t, half):
            codes, scales = wq
            rows = slice(t * P, (t + 1) * P)
            cols = slice(half * BANK, (half + 1) * BANK)
            nc.tensor.matmul_mx(
                out=banks[2 * t + half][:],
                lhsT=codes[:, rows].bitcast(FP8X4),
                lhsT_scale=scales[:, rows],
                rhs=v_c[a][:, cols].bitcast(FP8X4),
                rhs_scale=v_s[4 * a : P, cols],
                start=(a == 0),
                stop=(a == passes1 - 1),
            )

        def weather_product(b, t):
            h = ring.tile([P, S], F32, name="h", bufs=5)
            for half in range(2):
                cols = slice(half * BANK, (half + 1) * BANK)
                nc.vector.tensor_tensor(h[:, cols], banks[2 * t + half][:], we_sb[b][:, t, cols], MULT)
            return h

        def pick(h, picked, t, m0, m1):
            cols = list2[:, m0 // PER_COL : m1 // PER_COL]
            nc.vector.tensor_tensor(picked[:, t, :], h[:].indirect(cols), wgt_sb[:, m0:m1], MULT)

        def add_pond(x, picked, b, t):
            nc.scalar.activation(x[:, t, :], picked[:, t, :], IDENTITY, bias=pond_sb[:, b, t : t + 1])

        x_c = [keep.tile([P, M], U32, name=f"x_c{b}", align_bytes=64) for b in range(blocks)]
        x_s = [keep.tile([P, M], U8, name=f"x_s{b}", align_bytes=64) for b in range(blocks)]
        top_c = [keep.tile([P, M], U32, name=f"top_c{b}", align_bytes=64) for b in range(blocks)]
        top_s = [keep.tile([P, M], U8, name=f"top_s{b}", align_bytes=64) for b in range(blocks)]

        def quantize_x(x, b, m0, m1):
            grouped = ring.tile([P, (m1 - m0) * PACK], BF16, name="x_bf", align_bytes=64)
            nc.scalar.copy(
                out=grouped[:].rearrange("p (c i t) -> p c t i", i=4, t=PACK),
                in_=x.rearrange("p t (c i) -> p c t i", i=4),
            )
            quantize(grouped[:], x_c[b][:, m0:m1], x_s[b][:, m0:m1])

        def stage2_pass(a, bo, quarter):
            cols = slice(quarter * QUARTER, (quarter + 1) * QUARTER)
            bank = banks[2 * quarter + bo]
            for t in range(PACK):
                g = (a * blocks + bo) * PACK + t
                nc.tensor.matmul_mx(
                    out=bank[:, t * QUARTER : (t + 1) * QUARTER],
                    lhsT=w2_c[:, g * 2 * P : (g + 1) * 2 * P].bitcast(FP4X4),
                    lhsT_scale=w2_s[:, g * P : (g + 1) * P],
                    rhs=x_c[a][:, cols].bitcast(FP8X4),
                    rhs_scale=x_s[a][:, cols],
                    start=(a == 0 and t == 0),
                    stop=(a == blocks - 1 and t == PACK - 1),
                )

        nc.vector.tensor_copy(
            out=w2_c[:].rearrange("p (g t q e) -> p g t q e", t=PACK, q=P, e=2),
            in_=w2_raw[:].rearrange("p (g q t e) -> p g t q e", t=PACK, q=P, e=2),
        )
        w1_q = {(a, 0): quantize_weight(w1_raw[a, 0], f"w1q{a}0") for a in range(passes1)}
        nc.vector.tensor_copy(
            out=w2_s[:].rearrange("p (g t q) -> p g t q", t=PACK, q=P),
            in_=w2s_raw[:].rearrange("p (g q t) -> p g t q", t=PACK, q=P),
        )
        for t in range(PACK):
            nc.vector.memset(pages[t][:], 0.0)
        gather_table(0, 0, S)
        nc.vector.tensor_copy(v_s[:], tab_s[:].indirect(list1[:]))
        gather_table(1, 0, S)
        gather_table(2, 0, BANK)
        gather_table(2, BANK, S)
        for a in range(passes1):
            for t in range(PACK):
                for half in range(2):
                    stage1_pass(w1_q[a, 0], a, t, half)

        picked0 = we0[:, M:].rearrange("p (t j) -> p t j", t=PACK)[:, :, S - M :]
        hs = [weather_product(0, 0)]
        for t in range(PACK):
            if t + 1 < PACK:
                hs.append(weather_product(0, t + 1))
            if t >= 1:
                w1_q[t - 1, 1] = quantize_weight(w1_raw[t - 1, 1], f"w1q{t - 1}1")
            pick(hs[t], picked0, t, 0, M)
        for a in range(passes1):
            for t in range(PACK):
                for half in range(2):
                    stage1_pass(w1_q[a, 1], a, t, half)
        x0 = w1_raw[passes1 - 1, 1][:]
        for t in range(PACK):
            add_pond(x0, picked0, 0, t)
        quantize_x(x0, 0, 0, M)
        w3_q = [quantize_weight(w3_raw[0], "w3q0")]

        last = (PACK - 1) * PITCH + QUARTER
        picked1 = we1[:, QUARTER:].rearrange("p (t j) -> p t j", t=PACK)[:, :, S:]
        x1_first = keep.tile([P, PACK, HALF], F32, name="x1_first")
        x1 = [x1_first[:], we1[:, last : last + PACK * HALF].rearrange("p (t m) -> p t m", t=PACK)]
        hs = [weather_product(1, 0)]
        for t in range(PACK):
            if t + 1 < PACK:
                hs.append(weather_product(1, t + 1))
            pick(hs[t], picked1, t, 0, HALF)
            add_pond(x1[0], picked1, 1, t)
        for quarter in range(4):
            for bo in range(blocks):
                stage2_pass(0, bo, quarter)
        quantize_x(x1[0], 1, 0, HALF)
        for t in range(PACK):
            pick(hs[t], x1[1], t, HALF, M)
            add_pond(x1[1], x1[1], 1, t)
        quantize_x(x1[1], 1, HALF, M)
        w3_q.append(quantize_weight(w3_raw[1], "w3q1"))

        out_rows = out.rearrange("(p t) c -> t p c", t=PACK)
        for half in range(2):
            m0 = half * HALF
            tops = [ring.tile([P, HALF * PACK], BF16, name="top_bf", align_bytes=64) for bo in range(blocks)]
            for part in range(2):
                quarter = 2 * half + part
                for bo in range(blocks):
                    stage2_pass(1, bo, quarter)
                    if bo == 0:
                        x_part = x0[:, :, quarter * QUARTER : (quarter + 1) * QUARTER]
                    else:
                        x_part = x1[half][:, :, part * QUARTER : (part + 1) * QUARTER]
                    nc.vector.tensor_tensor(
                        tops[bo][:, part * BANK : (part + 1) * BANK].rearrange("p (c i t) -> p c t i", i=4, t=PACK),
                        banks[2 * quarter + bo][:].rearrange("p (t c i) -> p c t i", t=PACK, i=4),
                        x_part.rearrange("p t (c i) -> p c t i", i=4),
                        MAX,
                    )
            for bo in range(blocks):
                quantize(tops[bo][:], top_c[bo][:, m0 : m0 + HALF], top_s[bo][:, m0 : m0 + HALF])
            for t in range(PACK):
                bank = banks[4 * half + t]
                rows = slice(t * P, (t + 1) * P)
                for a in range(blocks):
                    codes, scales = w3_q[a]
                    nc.tensor.matmul_mx(
                        out=bank[:, 0:HALF],
                        lhsT=codes[:, rows].bitcast(FP8X4),
                        lhsT_scale=scales[:, rows],
                        rhs=top_c[a][:, m0 : m0 + HALF].bitcast(FP8X4),
                        rhs_scale=top_s[a][:, m0 : m0 + HALF],
                        start=(a == 0),
                        stop=(a == blocks - 1),
                    )
                y = ring.tile([P, HALF], F32, name="y", bufs=4)
                nc.scalar.activation(y[:], bank[:, 0:HALF], IDENTITY, bias=master_sb[:, t : t + 1])
                cols = list3[:, m0 // PER_COL : (m0 + HALF) // PER_COL]
                nc.vector.tensor_tensor(pages[t][:].indirect(cols), y[:], wgo_sb[:, m0 : m0 + HALF], MULT)
                if half == 1:
                    nc.sync.dma_start(out=out_rows[t], in_=pages[t][:])
